import numpy as np
CORES = [112,113,114,115,124,125,126,127]
N = 8
def setup_inputs(rng):
    return {"x": rng.standard_normal((N, 128, 128), dtype=np.float32)}
def reference(x):
    s = x.sum(axis=0, dtype=np.float64).astype(x.dtype)
    s = np.maximum(s, 0)
    return {"y": np.broadcast_to(s, (N,) + s.shape)}

from concourse.bass import DstId, RemoteDMATransfer
from concourse.mybir import AluOpType

Q = 32

SCRATCH = {
    "xs":   ("sbuf", [128, 128], "float32"),
    "land": ("sbuf", [128, 128], "float32"),
    "t0":   ("sbuf", [128, Q], "float32"),
    "t1":   ("sbuf", [128, Q], "float32"),
    "part": ("sbuf", [128, Q], "float32"),
    "peer": ("sbuf", [128, Q], "float32"),
    "tot":  ("sbuf", [128, Q], "float32"),
    "zero": ("sbuf", [128, Q], "float32"),
    "fin":  ("sbuf", [128, Q], "float32"),
    "res":  ("sbuf", [128, 128], "float32"),
}
SEMAPHORES = [
    "ld",
    "st",
    "sent",
    "got1",
    "got2",
    "got3",
    "vz", "va", "vp", "vt", "vf",
]

OWNER_ON_CHIP = (2, 3, 6, 7)


def rank_program(g, core, T, topo):
    chips = sorted({topo.chip(c) for c in T.cores})
    my_chip = topo.chip(core)
    if my_chip not in chips:
        return
    mate_chip = chips[0] if my_chip == chips[1] else chips[1]
    ranks_here = [c for c in T.cores if topo.chip(c) == my_chip]
    owners_here = [my_chip * 8 + k for k in OWNER_ON_CHIP]
    is_rank = core in ranks_here
    is_owner = core in owners_here
    if not (is_rank or is_owner):
        return
    S = T.sem
    sent = 0

    def dst(c):
        rid, pid, _se = topo.addr(c)
        return DstId(rid=rid, pnc=pid)

    def cols(q):
        return slice(q * Q, (q + 1) * Q)

    if is_rank:
        j = ranks_here.index(core)
        g.sync.dma_start(T.xs[:], T.x[:]).then_inc(S.ld, 16)
        g.wait_ge(S.ld, 16)
        transfers = []
        for q, o in enumerate(owners_here):
            if o == core:
                continue
            transfers.append(RemoteDMATransfer(
                dst_ids=[dst(o)], dma_engine_mask=0xF << (4 * q), remote_sem=S.got1,
                src=T.xs[:, cols(q)], dst=T.land[:, cols(j)]))
            sent += 4
        g.remote_dma_fused(transfers, local_sem=S.sent)

    if is_owner:
        q = owners_here.index(core)
        partner = mate_chip * 8 + OWNER_ON_CHIP[q]
        v = g.vector
        v.memset(T.zero[:], 0.0).then_inc(S.vz, 1)
        parts = [T.xs[:, cols(q)] if c == core else T.land[:, cols(i)] for i, c in enumerate(ranks_here)]
        if is_rank:
            v.wait_ge(S.ld, 16)
        v.wait_ge(S.got1, 4 * (len(ranks_here) - (1 if is_rank else 0)))
        v.tensor_tensor(T.t0[:], parts[0], parts[1], AluOpType.add).then_inc(S.va, 1)
        v.tensor_tensor(T.t1[:], parts[2], parts[3], AluOpType.add).then_inc(S.va, 1)
        v.wait_ge(S.va, 2)
        v.tensor_tensor(T.part[:], T.t0[:], T.t1[:], AluOpType.add).then_inc(S.vp, 1)

        g.wait_ge(S.vp, 1)
        rid, pid, _se = topo.addr(partner)
        g.remote_dma(T.peer[:], T.part[:], S.got2, S.sent, pid, rid, topo.mask(core, partner))
        sent += 8

        v.wait_ge(S.vp, 1)
        v.wait_ge(S.got2, 8)
        v.tensor_tensor(T.tot[:], T.part[:], T.peer[:], AluOpType.add).then_inc(S.vt, 1)
        v.wait_ge(S.vt, 1)
        v.wait_ge(S.vz, 1)
        fin = T.res[:, cols(q)] if is_rank else T.fin[:]
        v.tensor_tensor(fin, T.tot[:], T.zero[:], AluOpType.max).then_inc(S.vf, 1)

        g.wait_ge(S.vf, 1)
        to = [c for c in ranks_here if c != core]
        g.remote_dma_fused([RemoteDMATransfer(
            dst_ids=[dst(c) for c in to], dma_engine_mask=0xFFFF, remote_sem=S.got3,
            srcs=[fin], dsts=[T.res[:, cols(q)] for _c in to])], local_sem=S.sent)
        sent += 16

    if is_rank:
        if is_owner:
            g.sync.wait_ge(S.vf, 1)
        g.sync.wait_ge(S.got3, 16 * (4 - (1 if is_owner else 0)))
        g.sync.dma_start(T.y[:], T.res[:]).then_inc(S.st, 16)
        g.sync.wait_ge(S.st, 16)

    g.wait_ge(S.sent, sent)
